import numpy as np
import ml_dtypes


def mxq(x, axis, fmt="e4m3"):
    dtype, down = {"e4m3": (ml_dtypes.float8_e4m3fn, 7), "e5m2": (ml_dtypes.float8_e5m2, 14)}[fmt]
    v = np.moveaxis(np.asarray(x, np.float32).astype(ml_dtypes.bfloat16).astype(np.float64), axis, -1)
    blocks = v.reshape(v.shape[:-1] + (-1, 32))
    amax = np.abs(blocks).max(-1, keepdims=True)
    byte = np.maximum(np.where(amax > 0, np.frexp(amax)[1] - 1 + 127, 0) - down, 1)
    scale = np.exp2(byte - 127.0)
    codes = (blocks / scale).astype(np.float32).astype(dtype).astype(np.float64)
    return np.moveaxis((codes * scale).reshape(v.shape), -1, axis)


WIDE = False


def mx_kscale(k):
    if not WIDE:
        return np.ones(k)
    levels = np.array([10, -10, 5, -5, 0])
    if k % 512:
        return np.exp2(np.random.permutation(np.resize(levels, k // 32))).repeat(32)
    a = np.empty((k // 512, 16))
    for p in range(k // 512):
        a[p, :8] = np.random.permutation(np.resize(levels, 8))
        for g in range(8):
            far = levels[np.abs(levels - a[p, g]) >= 10]
            a[p, g + 8] = far[np.random.randint(len(far))]
    return np.exp2(a.ravel()).repeat(32)


def f64(x):
    return np.asarray(x).astype(np.float64)


def striped(idx):
    return np.tile(idx.reshape(-1, 16).T, (8, 1)).astype(np.uint16)


def unstriped(offs):
    return offs[:16].T.reshape(-1).astype(np.int64)


E2M1 = np.array([0.0, 0.5, 1.0, 1.5, 2.0, 3.0, 4.0, 6.0, -0.0, -0.5, -1.0, -1.5, -2.0, -3.0, -4.0, -6.0])


def pack_weight(w, fmt):
    k, n = w.shape
    w = f64(np.asarray(w, np.float32).astype(ml_dtypes.bfloat16)).reshape(k // 32, 32, n)
    amax = np.abs(w).max(1)
    if fmt == "e4m3":
        byte = np.frexp(amax)[1] - 1 + 127 - 7
    else:
        mant, ex = np.frexp(amax / 6.0)
        byte = np.where(mant > 0.5, ex, ex - 1) + 127
    byte = np.clip(np.where(amax > 0, byte, 1), 1, 254)
    scaled = (w * np.exp2(127.0 - byte)[:, None, :]).reshape(k, n).astype(np.float32)
    by_word = np.ascontiguousarray(scaled.reshape(k // 512, 128, 4, n).transpose(0, 1, 3, 2))
    if fmt == "e4m3":
        words = by_word.astype(ml_dtypes.float8_e4m3fn).view(np.uint8)
    else:
        c = by_word.astype(ml_dtypes.float4_e2m1fn).view(np.uint8) & 0xF
        words = (c[..., 0::2] | (c[..., 1::2] << 4)).reshape(k // 512, 128, 2 * n)
    return np.ascontiguousarray(words), np.ascontiguousarray(byte.astype(np.uint8).reshape(k // 512, 16, n))


def unpack_weight(words, scales, fmt):
    g, _, n = scales.shape
    words = np.ascontiguousarray(words).reshape(g, 128, n, -1)
    if fmt == "e4m3":
        vals = words.view(ml_dtypes.float8_e4m3fn).astype(np.float64)
    else:
        nib = np.empty((g, 128, n, 4), np.uint8)
        nib[..., 0::2] = words & 0xF
        nib[..., 1::2] = words >> 4
        vals = E2M1[nib]
    vals = vals * np.repeat(np.exp2(scales.astype(np.float64) - 127.0), 8, axis=1)[..., None]
    return vals.transpose(0, 1, 3, 2).reshape(g * 512, n)


def gelu(v):
    return 0.5 * v * (1.0 + np.tanh(np.sqrt(2.0 / np.pi) * (v + 0.044715 * v**3)))


def striped8(idx):
    return np.concatenate([v.reshape(-1, 16).T for v in idx]).astype(np.uint16)


def unstriped8(offs):
    return np.stack([offs[16 * g:16 * g + 16].T.reshape(-1) for g in range(8)]).astype(np.int64)


def runs(v, idx8):
    k = np.arange(v.shape[0])
    return v[k[:, None], idx8[k % 512 // 64]]


K, H, N, T, S, P = 1536, 1024, 768, 2048, 1024, 512

def setup_inputs():
    n = np.random.standard_normal
    s = mx_kscale(K)[:, None]
    u = mx_kscale(H)[:, None]
    d = {}
    d["tab_words"], d["tab_scales"] = pack_weight(n((K, T)) * s, "e4m3")
    d["offs"] = striped8(np.stack([np.random.permutation(T)[:S] for _ in range(8)]))
    d["pos1"] = striped(np.random.permutation(S)[:P])
    d["pos2"] = striped(np.random.permutation(S)[:P])
    d["w1"] = (1.5 * n((K, H)) / s / K ** 0.5).astype(np.float32)
    d["lift"] = (2.5 * np.sign(n(H)) * np.exp(0.3 * n(H))).astype(np.float32)
    d["gain"] = (u[:, 0] * np.exp(0.3 * n(H))).astype(np.float32)
    d["w4_words"], d["w4_scales"] = pack_weight(0.4 * n((H, N)) / u / H ** 0.5, "e2m1")
    d["cap"] = (0.4 + 0.6 * n((N, P))).astype(np.float32)
    return d

def reference(tab_words, tab_scales, offs, pos1, pos2, w1, lift, gain, w4_words, w4_scales, cap):
    v = runs(unpack_weight(tab_words, tab_scales, "e4m3"), unstriped8(offs))
    h = np.abs(mxq(f64(w1), 0, "e4m3").T @ v)
    l = f64(lift)[:, None] * np.log(1.0 + h)
    z = f64(gain)[:, None] * (h[:, unstriped(pos1)] + l[:, unstriped(pos2)])
    w4 = unpack_weight(w4_words, w4_scales, "e2m1")
    y = w4.T @ mxq(z, 0, "e4m3")
    return np.minimum(y, f64(cap))

@@ -1,0 +1,296 @@
+from contextlib import ExitStack
+
+import concourse.mybir as mybir
+
+K, H, N, T, S, M = 1536, 1024, 768, 2048, 1024, 512
+FLOPS = 2 * K * H * S + 2 * H * N * M
+
+F32 = mybir.dt.float32
+BF16 = mybir.dt.bfloat16
+I32 = mybir.dt.int32
+U32 = mybir.dt.uint32
+U16 = mybir.dt.uint16
+U8 = mybir.dt.uint8
+FP8X4 = mybir.dt.float8_e4m3fn_x4
+FP4X4 = mybir.dt.float4_e2m1fn_x4
+ALU = mybir.AluOpType
+ACT = mybir.ActivationFunctionType
+
+P = 128
+PACK = 4
+K_PASS = P * PACK
+BANK = 512
+PASSES1 = K // K_PASS
+PASSES2 = H // K_PASS
+HALVES = S // BANK
+N_TILES = N // P
+
+
+def tile_list_drum_phase_scores_kernel(
+    tc, tab_words, tab_scales, offs, pos1, pos2, w1, lift, gain, w4_words, w4_scales, cap, out
+):
+    nc = tc.nc
+    with ExitStack() as ctx:
+        keep = ctx.enter_context(tc.tile_pool(name="keep", bufs=1))
+        ring = ctx.enter_context(tc.tile_pool(name="ring", bufs=3))
+        psum = ctx.enter_context(tc.psum_pool(name="psum", bufs=8))
+
+        def held(shape, dtype, name):
+            return keep.tile(shape, dtype, name=name, align_bytes=64)
+
+        offs_sb = held([P, S // 16], U16, "offs_sb")
+        pos1_sb = held([P, M // 16], U16, "pos1_sb")
+        pos2_sb = held([P, M // 16], U16, "pos2_sb")
+        picked_scales = held([P, S], U8, "picked_scales")
+        v_scales = held([P, S], U8, "v_scales")
+        table = {}
+        w_raw = {}
+        v_codes = [held([P, S], U32, "v_codes%d" % a) for a in range(PASSES1)]
+        w_keys = [(b, a) for b in range(PASSES2) for a in range(PASSES1)]
+        w_codes = {key: held([P, K_PASS], U32, "w_codes%d%d" % key) for key in w_keys}
+        w_scales = {key: held([P, K_PASS], U8, "w_scales%d%d" % key) for key in w_keys}
+        gain_sb = held([P, PASSES2, PACK], F32, "gain_sb")
+        lift_sb = held([P, PASSES2, PACK], F32, "lift_sb")
+        w4_scale_sb = held([P, PASSES2, N], U8, "w4_scale_sb")
+        sums = [held([P, PACK, M], F32, "sums%d" % b) for b in range(PASSES2)]
+        z_codes = [held([P, M], U32, "z_codes%d" % b) for b in range(PASSES2)]
+        z_scales = [held([P, M], U8, "z_scales%d" % b) for b in range(PASSES2)]
+
+
+        def streamed(shape, dtype, slot):
+            return keep.tile(shape, dtype, name="slot_" + slot, align_bytes=64)
+
+        def load_table(a):
+            table[a] = streamed([P, T], I32, "cbc"[a])
+            nc.sync.dma_start(table[a][:], tab_words[a].rearrange("p t i -> p (t i)").bitcast(I32))
+
+        def load_w1(b, a):
+            if (b, a) == (1, 1):
+                w_raw[b, a] = streamed([P, PACK, K_PASS], F32, "b")
+            else:
+                w_raw[b, a] = w_stage[(a + b) % 2 if b == 0 or a == 0 else 0]
+            rows = w1[K_PASS * a : K_PASS * (a + 1), K_PASS * b : K_PASS * (b + 1)]
+            nc.sync.dma_start(w_raw[b, a][:], rows.rearrange("(p j) c -> p j c", j=PACK))
+
+        scale_window = streamed([P, T], U8, "b")
+        lift_stage = streamed([P, PASSES2, PACK], F32, "c")
+        w_stage = [held([P, PACK, K_PASS], F32, "w_stage%d" % i) for i in range(2)]
+        gain_stage = w_stage[1][:, 0, 0 : PASSES2 * PACK].rearrange("p (b t) -> p b t", t=PACK)
+        warm = held([P, 1], F32, "warm")
+        nc.vector.memset(scale_window[:].bitcast(I32), 0)
+        nc.gpsimd.memset(warm[:], 1.0)
+        nc.gpsimd.memset(w4_scale_sb[:].rearrange("p b n -> p (b n)").bitcast(I32), 0)
+        nc.scalar.activation(warm[:], warm[:], ACT.Ln)
+        nc.sync.dma_start(lift_stage[:], lift.rearrange("(b p t) -> p b t", p=P, t=PACK))
+        nc.sync.dma_start(gain_stage, gain.rearrange("(b p t) -> p b t", p=P, t=PACK))
+        nc.sync.dma_start(offs_sb[:], offs)
+        nc.sync.dma_start(pos2_sb[:], pos2)
+        nc.sync.dma_start(pos1_sb[:], pos1)
+        nc.vector.tensor_copy(lift_sb[:], lift_stage[:])
+        nc.vector.tensor_copy(gain_sb[:], gain_stage)
+        load_w1(0, 0)
+        window32 = scale_window[:].bitcast(I32)
+        scales32 = tab_scales.bitcast(I32)
+        for r in range(2):
+            nc.sync.dma_start(window32[r:P:8, :], scales32[0:3:2, r:16:2, :].rearrange("a g w -> g a w"))
+            nc.sync.dma_start(window32[4 + r : P : 16, :], scales32[1, r:16:2, :])
+        load_table(0)
+        load_w1(0, 1)
+        load_table(1)
+
+        def gather_table(a, lo, hi):
+            nc.vector.tensor_copy(
+                v_codes[a][:, lo:hi], table[a][:].bitcast(U32).indirect(offs_sb[:, lo // 16 : hi // 16])
+            )
+
+        nc.vector.tensor_copy(picked_scales[:], scale_window[:].indirect(offs_sb[:]))
+        picked32 = picked_scales[:].bitcast(I32)
+        planes32 = v_scales[:].bitcast(I32)
+        nc.vector.tensor_copy(planes32, picked32)
+        for r in range(2):
+            nc.sync.dma_start(planes32[2 + r : P - 14 + r : 4, :], picked32[16 + r : P : 4, :])
+        for d in range(4):
+            nc.gpsimd.dma_start(
+                w4_scale_sb[:].bitcast(I32)[32 * d : 32 * d + 4],
+                w4_scales.bitcast(I32)[:, 4 * d : 4 * d + 4, :].rearrange("b r w -> r b w"),
+            )
+
+        probe = held([P, 16], F32, "probe")
+        probe8 = held([P, 4], U8, "probe8")
+        nc.gpsimd.tensor_copy(probe8[:], picked_scales[:, 0:4])
+        grouped = {}
+
+        def cast_w1(copy, b, a, lo, hi):
+            if (b, a) not in grouped:
+                grouped[b, a] = ring.tile([P, PACK * K_PASS], BF16, name="grouped", align_bytes=64)
+            dst = grouped[b, a][:].rearrange("p (t m j) -> p m j t", t=PACK, j=PACK)
+            src = w_raw[b, a][:].rearrange("p j (m t) -> p m j t", t=PACK)
+            copy(dst[:, lo:hi], src[:, lo:hi])
+
+        def quantize_w1(b, a):
+            nc.vector.quantize_mx(out=w_codes[b, a][:].bitcast(FP8X4), scales=w_scales[b, a][:], in_=grouped[b, a][:])
+
+        banks = {}
+
+        def first_product(b, t, half, a):
+            if a == 0:
+                banks[b, t, half] = psum.tile([P, BANK], F32, name="bank")
+            rows = slice(P * t, P * (t + 1))
+            cols = slice(BANK * half, BANK * (half + 1))
+            nc.tensor.matmul_mx(
+                out=banks[b, t, half][:],
+                lhsT=w_codes[b, a][:, rows].bitcast(FP8X4),
+                lhsT_scale=w_scales[b, a][:, rows],
+                rhs=v_codes[a][:, cols].bitcast(FP8X4),
+                rhs_scale=v_scales[4 * a : P, cols],
+                start=(a == 0),
+                stop=(a == (PASSES1 - 1 if b == 0 else 1)),
+            )
+
+        strength = {}
+        second = {}
+        lifted = {}
+
+        def absolute(b, t):
+            strength[b, t] = ring.tile([P, S], F32, name="strength", bufs=4)
+            for half in range(HALVES):
+                nc.scalar.activation(strength[b, t][:, BANK * half : BANK * (half + 1)], banks[b, t, half][:], ACT.Abs)
+
+        def pick_second(b, t):
+            second[b, t] = ring.tile([P, M], F32, name="second")
+            nc.vector.tensor_copy(second[b, t][:], strength[b, t][:].indirect(pos2_sb[:]))
+
+        def compress(b, t):
+            logged = ring.tile([P, M], F32, name="logged")
+            nc.scalar.activation(logged[:], second[b, t][:], ACT.Ln, bias=1.0)
+            lifted[b, t] = ring.tile([P, M], F32, name="lifted")
+            nc.scalar.activation(lifted[b, t][:], logged[:], ACT.Copy, scale=lift_sb[:, b, t : t + 1])
+
+        def pick_first(b, t):
+            nc.vector.tensor_tensor(sums[b][:, t, :], strength[b, t][:].indirect(pos1_sb[:]), lifted[b, t][:], ALU.add)
+
+        z_bf = {}
+
+        def weigh(b):
+            z_bf[b] = ring.tile([P, M * PACK], BF16, name="z_bf", bufs=2, align_bytes=64)
+            nc.vector.tensor_tensor(
+                z_bf[b][:].rearrange("p (c i t) -> p c t i", i=4, t=PACK),
+                sums[b][:].rearrange("p t (c i) -> p c t i", i=4),
+                gain_sb[:, b, :].unsqueeze(1).unsqueeze(3).to_broadcast([P, M // 4, PACK, 4]),
+                ALU.mult,
+            )
+
+        def weigh_on_scalar(b, t):
+            if t == 0:
+                z_bf[b, "rows"] = held([P, PACK, M], BF16, "z_rows")
+            nc.scalar.activation(z_bf[b, "rows"][:, t, :], sums[b][:, t, :], ACT.Copy, scale=gain_sb[:, b, t : t + 1])
+
+        def interleave(b):
+            z_bf[b] = ring.tile([P, M * PACK], BF16, name="z_bf", bufs=2, align_bytes=64)
+            nc.vector.tensor_copy(
+                z_bf[b][:].rearrange("p (c i t) -> p c t i", i=4, t=PACK),
+                z_bf[b, "rows"][:].rearrange("p t (c i) -> p c t i", i=4),
+            )
+
+        def quantize_z(b):
+            nc.vector.quantize_mx(out=z_codes[b][:].bitcast(FP8X4), scales=z_scales[b][:], in_=z_bf[b][:])
+
+        gather_table(0, 0, S)
+        cast_w1(nc.scalar.copy, 0, 0, 0, P)
+        load_w1(0, 2)
+        load_table(2)
+        quantize_w1(0, 0)
+        cast_w1(nc.scalar.copy, 0, 1, 0, P)
+        load_w1(1, 0)
+        load_w1(1, 1)
+        quantize_w1(0, 1)
+        gather_table(1, 0, S)
+        nc.gpsimd.tensor_copy(probe[:, 0:1], w_raw[0, 2][:, 3, 511:512])
+        cast_w1(nc.scalar.copy, 0, 2, 0, P)
+        load_w1(1, 2)
+        quantize_w1(0, 2)
+        gather_table(2, 0, BANK)
+        gather_table(2, BANK, S)
+        for pair in range(0, PACK, 2):
+            for a in range(PASSES1):
+                for t in (pair, pair + 1):
+                    for half in range(HALVES):
+                        first_product(0, t, half, a)
+
+        half_rows = P // 2
+        cast_w1(nc.scalar.copy, 1, 0, 0, half_rows)
+        absolute(0, 0)
+        pick_second(0, 0)
+        absolute(0, 1)
+        pick_second(0, 1)
+        compress(0, 0)
+        pick_first(0, 0)
+        cast_w1(nc.scalar.copy, 1, 0, half_rows, P)
+        w4_sb = streamed([P, PASSES2, 2 * N], U8, "c")
+        nc.sync.dma_start(w4_sb[:].bitcast(I32), w4_words.bitcast(I32).rearrange("b p w -> p b w"))
+        cap_rows = cap.rearrange("(j p) m -> p j m", p=P)
+        cap_sb = []
+        for j in range(0, N_TILES, 3):
+            cap_sb.append(w_stage[1][:, 0:3, :] if j == 0 else streamed([P, 3, M], F32, "b")[:])
+            nc.sync.dma_start(cap_sb[-1], cap_rows[:, j : j + 3, :])
+        quantize_w1(1, 0)
+        absolute(0, 2)
+        cast_w1(nc.vector.tensor_copy, 1, 2, 0, P)
+        pick_second(0, 2)
+        compress(0, 1)
+        pick_first(0, 1)
+        quantize_w1(1, 2)
+        cast_w1(nc.scalar.copy, 1, 1, 0, half_rows)
+        absolute(0, 3)
+        pick_second(0, 3)
+        cast_w1(nc.scalar.copy, 1, 1, half_rows, P)
+        quantize_w1(1, 1)
+        compress(0, 2)
+        pick_first(0, 2)
+        compress(0, 3)
+        pick_first(0, 3)
+        for a in (0, 2, 1):
+            for t in range(PACK):
+                for half in range(HALVES):
+                    first_product(1, t, half, a)
+        absolute(1, 0)
+        pick_second(1, 0)
+        absolute(1, 1)
+        pick_second(1, 1)
+        compress(1, 0)
+        pick_first(1, 0)
+        absolute(1, 2)
+        pick_second(1, 2)
+        compress(1, 1)
+        weigh_on_scalar(0, 0)
+        weigh_on_scalar(0, 1)
+        pick_first(1, 1)
+        absolute(1, 3)
+        pick_second(1, 3)
+        compress(1, 2)
+        weigh_on_scalar(0, 2)
+        weigh_on_scalar(0, 3)
+        pick_first(1, 2)
+        compress(1, 3)
+        interleave(0)
+        pick_first(1, 3)
+        quantize_z(0)
+        weigh(1)
+        quantize_z(1)
+
+        scores = [psum.tile([P, M], F32, name="bank") for j in range(N_TILES)]
+        for b in range(PASSES2):
+            for j in range(N_TILES):
+                nc.tensor.matmul_mx(
+                    out=scores[j][:],
+                    lhsT=w4_sb[:, b, 2 * P * j : 2 * P * (j + 1)].bitcast(FP4X4),
+                    lhsT_scale=w4_scale_sb[:, b, P * j : P * (j + 1)],
+                    rhs=z_codes[b][:].bitcast(FP8X4),
+                    rhs_scale=z_scales[b][:],
+                    start=(b == 0),
+                    stop=(b == PASSES2 - 1),
+                )
+        for j in range(N_TILES):
+            result = ring.tile([P, M], F32, name="result", bufs=N_TILES)
+            nc.vector.tensor_tensor(result[:], scores[j][:], cap_sb[j // 3][:, j % 3, :], ALU.min)
+            nc.sync.dma_start(out[P * j : P * (j + 1), :], result[:])

@@ -49,10 +49,15 @@ def tile_list_drum_phase_scores_kernel(
         w_keys = [(b, a) for b in range(PASSES2) for a in range(PASSES1)]
         w_codes = {key: held([P, K_PASS], U32, "w_codes%d%d" % key) for key in w_keys}
         w_scales = {key: held([P, K_PASS], U8, "w_scales%d%d" % key) for key in w_keys}
-        gain_sb = held([P, PASSES2, PACK], F32, "gain_sb")
-        lift_sb = held([P, PASSES2, PACK], F32, "lift_sb")
+        factor_rows = held([P, P], F32, "factor_rows")
+        factor_dealt = held([P, P], F32, "factor_dealt")
+        factors = held([P, PACK, PASSES2, 16], F32, "factors")
+        products = held([P, PACK, PASSES2], F32, "products")
+        gain_wide = [held([P, PACK, M], F32, "gain_wide%d" % b) for b in range(PASSES2)]
+        product_wide = [held([P, PACK, M], F32, "product_wide%d" % b) for b in range(PASSES2)]
         w4_scale_sb = held([P, PASSES2, N], U8, "w4_scale_sb")
-        sums = [held([P, PACK, M], F32, "sums%d" % b) for b in range(PASSES2)]
+        charge = [held([P, PACK, M], F32, "charge%d" % b) for b in range(PASSES2)]
+        develop = [held([P, PACK, M], F32, "develop%d" % b) for b in range(PASSES2)]
         z_codes = [held([P, M], U32, "z_codes%d" % b) for b in range(PASSES2)]
         z_scales = [held([P, M], U8, "z_scales%d" % b) for b in range(PASSES2)]
 
@@ -73,22 +78,27 @@ def tile_list_drum_phase_scores_kernel(
             nc.sync.dma_start(w_raw[b, a][:], rows.rearrange("(p j) c -> p j c", j=PACK))
 
         scale_window = streamed([P, T], U8, "b")
-        lift_stage = streamed([P, PASSES2, PACK], F32, "c")
+        warm = streamed([P, 2], F32, "c")
         w_stage = [held([P, PACK, K_PASS], F32, "w_stage%d" % i) for i in range(2)]
-        gain_stage = w_stage[1][:, 0, 0 : PASSES2 * PACK].rearrange("p (b t) -> p b t", t=PACK)
-        warm = held([P, 1], F32, "warm")
+        warm_bias = w_stage[1][:, 0, 0:1]
+        nc.vector.memset(warm[:, 0:1], 1.0)
+        nc.vector.memset(factor_rows[:], 0.0)
         nc.vector.memset(scale_window[:].bitcast(I32), 0)
-        nc.gpsimd.memset(warm[:], 1.0)
+        nc.vector.memset(warm[:, 1:2], 1.0)
+        nc.gpsimd.memset(warm_bias, 1.0)
         nc.gpsimd.memset(w4_scale_sb[:].rearrange("p b n -> p (b n)").bitcast(I32), 0)
-        nc.scalar.activation(warm[:], warm[:], ACT.Ln)
-        nc.sync.dma_start(lift_stage[:], lift.rearrange("(b p t) -> p b t", p=P, t=PACK))
-        nc.sync.dma_start(gain_stage, gain.rearrange("(b p t) -> p b t", p=P, t=PACK))
+        nc.scalar.activation(warm[:], warm[:], ACT.Ln, bias=warm_bias)
+        load_w1(0, 0)
         nc.sync.dma_start(offs_sb[:], offs)
         nc.sync.dma_start(pos2_sb[:], pos2)
         nc.sync.dma_start(pos1_sb[:], pos1)
-        nc.vector.tensor_copy(lift_sb[:], lift_stage[:])
-        nc.vector.tensor_copy(gain_sb[:], gain_stage)
-        load_w1(0, 0)
+        for v, vector in enumerate((gain, lift)):
+            nc.sync.dma_start(factor_rows[v:P:16, :], vector.rearrange("(b q c) -> q b c", b=PASSES2, c=P))
+        nc.scalar.copy(
+            factor_dealt[:].rearrange("p (t i) -> p t i", t=PACK), factor_rows[:].rearrange("p (i t) -> p t i", t=PACK)
+        )
+        nc.vector.transpose(factors[:].rearrange("p t b v -> p (t b v)"), factor_dealt[:])
+        nc.vector.tensor_tensor(products[:], factors[:, :, :, 0], factors[:, :, :, 1], ALU.mult)
         window32 = scale_window[:].bitcast(I32)
         scales32 = tab_scales.bitcast(I32)
         for r in range(2):
@@ -116,8 +126,6 @@ def tile_list_drum_phase_scores_kernel(
             )
 
         probe = held([P, 16], F32, "probe")
-        probe8 = held([P, 4], U8, "probe8")
-        nc.gpsimd.tensor_copy(probe8[:], picked_scales[:, 0:4])
         grouped = {}
 
         def cast_w1(copy, b, a, lo, hi):
@@ -144,52 +152,28 @@ def tile_list_drum_phase_scores_kernel(
                 rhs=v_codes[a][:, cols].bitcast(FP8X4),
                 rhs_scale=v_scales[4 * a : P, cols],
                 start=(a == 0),
-                stop=(a == (PASSES1 - 1 if b == 0 else 1)),
+                stop=(a == PASSES1 - 1),
             )
 
-        strength = {}
-        second = {}
-        lifted = {}
-
-        def absolute(b, t):
-            strength[b, t] = ring.tile([P, S], F32, name="strength", bufs=4)
+        def pick_pairs(b, t):
+            strength = ring.tile([P, S], F32, name="strength", bufs=4)
             for half in range(HALVES):
-                nc.scalar.activation(strength[b, t][:, BANK * half : BANK * (half + 1)], banks[b, t, half][:], ACT.Abs)
-
-        def pick_second(b, t):
-            second[b, t] = ring.tile([P, M], F32, name="second")
-            nc.vector.tensor_copy(second[b, t][:], strength[b, t][:].indirect(pos2_sb[:]))
-
-        def compress(b, t):
-            logged = ring.tile([P, M], F32, name="logged")
-            nc.scalar.activation(logged[:], second[b, t][:], ACT.Ln, bias=1.0)
-            lifted[b, t] = ring.tile([P, M], F32, name="lifted")
-            nc.scalar.activation(lifted[b, t][:], logged[:], ACT.Copy, scale=lift_sb[:, b, t : t + 1])
-
-        def pick_first(b, t):
-            nc.vector.tensor_tensor(sums[b][:, t, :], strength[b, t][:].indirect(pos1_sb[:]), lifted[b, t][:], ALU.add)
+                nc.scalar.activation(strength[:, BANK * half : BANK * (half + 1)], banks[b, t, half][:], ACT.Abs)
+            if t == 0 and b == 0:
+                nc.gpsimd.tensor_copy(probe[:, b : b + 1], strength[:, S - 1 : S])
+            logged = ring.tile([P, S], F32, name="logged")
+            nc.scalar.activation(logged[:], strength[:], ACT.Ln, bias=1.0)
+            nc.vector.tensor_tensor(charge[b][:, t, :], strength[:].indirect(pos1_sb[:]), gain_wide[b][:, t, :], ALU.mult)
+            nc.vector.tensor_tensor(develop[b][:, t, :], logged[:].indirect(pos2_sb[:]), product_wide[b][:, t, :], ALU.mult)
 
         z_bf = {}
 
-        def weigh(b):
-            z_bf[b] = ring.tile([P, M * PACK], BF16, name="z_bf", bufs=2, align_bytes=64)
+        def join(b):
             nc.vector.tensor_tensor(
                 z_bf[b][:].rearrange("p (c i t) -> p c t i", i=4, t=PACK),
-                sums[b][:].rearrange("p t (c i) -> p c t i", i=4),
-                gain_sb[:, b, :].unsqueeze(1).unsqueeze(3).to_broadcast([P, M // 4, PACK, 4]),
-                ALU.mult,
-            )
-
-        def weigh_on_scalar(b, t):
-            if t == 0:
-                z_bf[b, "rows"] = held([P, PACK, M], BF16, "z_rows")
-            nc.scalar.activation(z_bf[b, "rows"][:, t, :], sums[b][:, t, :], ACT.Copy, scale=gain_sb[:, b, t : t + 1])
-
-        def interleave(b):
-            z_bf[b] = ring.tile([P, M * PACK], BF16, name="z_bf", bufs=2, align_bytes=64)
-            nc.vector.tensor_copy(
-                z_bf[b][:].rearrange("p (c i t) -> p c t i", i=4, t=PACK),
-                z_bf[b, "rows"][:].rearrange("p t (c i) -> p c t i", i=4),
+                charge[b][:].rearrange("p t (c i) -> p c t i", i=4),
+                develop[b][:].rearrange("p t (c i) -> p c t i", i=4),
+                ALU.add,
             )
 
         def quantize_z(b):
@@ -205,27 +189,27 @@ def tile_list_drum_phase_scores_kernel(
         load_w1(1, 1)
         quantize_w1(0, 1)
         gather_table(1, 0, S)
-        nc.gpsimd.tensor_copy(probe[:, 0:1], w_raw[0, 2][:, 3, 511:512])
         cast_w1(nc.scalar.copy, 0, 2, 0, P)
         load_w1(1, 2)
         quantize_w1(0, 2)
         gather_table(2, 0, BANK)
         gather_table(2, BANK, S)
-        for pair in range(0, PACK, 2):
-            for a in range(PASSES1):
-                for t in (pair, pair + 1):
-                    for half in range(HALVES):
-                        first_product(0, t, half, a)
+        def first_products(b):
+            for pair in range(0, PACK, 2):
+                for a in range(PASSES1):
+                    for t in (pair, pair + 1):
+                        for half in range(HALVES):
+                            first_product(b, t, half, a)
 
-        half_rows = P // 2
-        cast_w1(nc.scalar.copy, 1, 0, 0, half_rows)
-        absolute(0, 0)
-        pick_second(0, 0)
-        absolute(0, 1)
-        pick_second(0, 1)
-        compress(0, 0)
-        pick_first(0, 0)
-        cast_w1(nc.scalar.copy, 1, 0, half_rows, P)
+        first_products(0)
+
+        for t in range(PACK):
+            nc.scalar.copy(gain_wide[0][:, t, :], factors[:, t, 0, 0:1].to_broadcast([P, M]))
+            nc.scalar.copy(product_wide[0][:, t, :], products[:, t, 0:1].to_broadcast([P, M]))
+
+        pick_pairs(0, 0)
+        pick_pairs(0, 1)
+        cast_w1(nc.vector.tensor_copy, 1, 0, 0, P)
         w4_sb = streamed([P, PASSES2, 2 * N], U8, "c")
         nc.sync.dma_start(w4_sb[:].bitcast(I32), w4_words.bitcast(I32).rearrange("b p w -> p b w"))
         cap_rows = cap.rearrange("(j p) m -> p j m", p=P)
@@ -234,48 +218,28 @@ def tile_list_drum_phase_scores_kernel(
             cap_sb.append(w_stage[1][:, 0:3, :] if j == 0 else streamed([P, 3, M], F32, "b")[:])
             nc.sync.dma_start(cap_sb[-1], cap_rows[:, j : j + 3, :])
         quantize_w1(1, 0)
-        absolute(0, 2)
-        cast_w1(nc.vector.tensor_copy, 1, 2, 0, P)
-        pick_second(0, 2)
-        compress(0, 1)
-        pick_first(0, 1)
-        quantize_w1(1, 2)
-        cast_w1(nc.scalar.copy, 1, 1, 0, half_rows)
-        absolute(0, 3)
-        pick_second(0, 3)
-        cast_w1(nc.scalar.copy, 1, 1, half_rows, P)
+        pick_pairs(0, 2)
+        cast_w1(nc.scalar.copy, 1, 1, 0, P)
         quantize_w1(1, 1)
-        compress(0, 2)
-        pick_first(0, 2)
-        compress(0, 3)
-        pick_first(0, 3)
-        for a in (0, 2, 1):
-            for t in range(PACK):
-                for half in range(HALVES):
-                    first_product(1, t, half, a)
-        absolute(1, 0)
-        pick_second(1, 0)
-        absolute(1, 1)
-        pick_second(1, 1)
-        compress(1, 0)
-        pick_first(1, 0)
-        absolute(1, 2)
-        pick_second(1, 2)
-        compress(1, 1)
-        weigh_on_scalar(0, 0)
-        weigh_on_scalar(0, 1)
-        pick_first(1, 1)
-        absolute(1, 3)
-        pick_second(1, 3)
-        compress(1, 2)
-        weigh_on_scalar(0, 2)
-        weigh_on_scalar(0, 3)
-        pick_first(1, 2)
-        compress(1, 3)
-        interleave(0)
-        pick_first(1, 3)
+        pick_pairs(0, 3)
+        cast_w1(nc.vector.tensor_copy, 1, 2, 0, P // 2)
+        cast_w1(nc.scalar.copy, 1, 2, P // 2, P)
+        quantize_w1(1, 2)
+        first_products(1)
+        for t in range(PACK):
+            nc.scalar.copy(product_wide[1][:, t, :], products[:, t, 1:2].to_broadcast([P, M]))
+        for pair in range(0, PACK, 2):
+            nc.vector.tensor_copy(
+                gain_wide[1][:, pair : pair + 2, :], factors[:, pair : pair + 2, 1, 0:1].to_broadcast([P, 2, M])
+            )
+        z_bf[0] = grouped[1, 2]
+        z_bf[1] = ring.tile([P, M * PACK], BF16, name="grouped", align_bytes=64)
+        join(0)
+        pick_pairs(1, 0)
         quantize_z(0)
-        weigh(1)
+        for t in range(1, PACK):
+            pick_pairs(1, t)
+        join(1)
         quantize_z(1)
 
         scores = [psum.tile([P, M], F32, name="bank") for j in range(N_TILES)]

@@ -88,13 +88,13 @@ def tile_list_drum_phase_scores_kernel(
         nc.gpsimd.memset(warm_bias, 1.0)
         nc.gpsimd.memset(w4_scale_sb[:].rearrange("p b n -> p (b n)").bitcast(I32), 0)
         nc.scalar.activation(warm[:], warm[:], ACT.Ln, bias=warm_bias)
-        load_w1(0, 0)
         nc.sync.dma_start(offs_sb[:], offs)
         nc.sync.dma_start(pos2_sb[:], pos2)
         nc.sync.dma_start(pos1_sb[:], pos1)
+        load_w1(0, 0)
         for v, vector in enumerate((gain, lift)):
             nc.sync.dma_start(factor_rows[v:P:16, :], vector.rearrange("(b q c) -> q b c", b=PASSES2, c=P))
-        nc.scalar.copy(
+        nc.vector.tensor_copy(
             factor_dealt[:].rearrange("p (t i) -> p t i", t=PACK), factor_rows[:].rearrange("p (i t) -> p t i", t=PACK)
         )
         nc.vector.transpose(factors[:].rearrange("p t b v -> p (t b v)"), factor_dealt[:])
@@ -155,40 +155,65 @@ def tile_list_drum_phase_scores_kernel(
                 stop=(a == PASSES1 - 1),
             )
 
-        def pick_pairs(b, t):
-            strength = ring.tile([P, S], F32, name="strength", bufs=4)
+        strength = {}
+        logged = {}
+
+        def leave_psum(b, t):
+            strength[b, t] = ring.tile([P, S], F32, name="strength", bufs=4)
             for half in range(HALVES):
-                nc.scalar.activation(strength[:, BANK * half : BANK * (half + 1)], banks[b, t, half][:], ACT.Abs)
-            if t == 0 and b == 0:
-                nc.gpsimd.tensor_copy(probe[:, b : b + 1], strength[:, S - 1 : S])
-            logged = ring.tile([P, S], F32, name="logged")
-            nc.scalar.activation(logged[:], strength[:], ACT.Ln, bias=1.0)
-            nc.vector.tensor_tensor(charge[b][:, t, :], strength[:].indirect(pos1_sb[:]), gain_wide[b][:, t, :], ALU.mult)
-            nc.vector.tensor_tensor(develop[b][:, t, :], logged[:].indirect(pos2_sb[:]), product_wide[b][:, t, :], ALU.mult)
+                nc.scalar.activation(strength[b, t][:, BANK * half : BANK * (half + 1)], banks[b, t, half][:], ACT.Abs)
+            if t == 0:
+                nc.gpsimd.tensor_copy(probe[:, b : b + 1], strength[b, t][:, S - 1 : S])
+            logged[b, t] = ring.tile([P, S], F32, name="logged")
+            nc.scalar.activation(logged[b, t][:], strength[b, t][:], ACT.Ln, bias=1.0)
+
+        def pick_charge(b, t, lo, hi):
+            picked = strength[b, t][:].indirect(pos1_sb[:, lo // 16 : hi // 16])
+            nc.vector.tensor_tensor(charge[b][:, t, lo:hi], picked, gain_wide[b][:, t, lo:hi], ALU.mult)
+
+        def pick_develop(b, t, lo, hi):
+            picked = logged[b, t][:].indirect(pos2_sb[:, lo // 16 : hi // 16])
+            nc.vector.tensor_tensor(develop[b][:, t, lo:hi], picked, product_wide[b][:, t, lo:hi], ALU.mult)
+
+        def pick_pairs(b, t):
+            leave_psum(b, t)
+            pick_charge(b, t, 0, M)
+            pick_develop(b, t, 0, M)
 
         z_bf = {}
 
-        def join(b):
+        def join(b, lo, hi):
             nc.vector.tensor_tensor(
-                z_bf[b][:].rearrange("p (c i t) -> p c t i", i=4, t=PACK),
-                charge[b][:].rearrange("p t (c i) -> p c t i", i=4),
-                develop[b][:].rearrange("p t (c i) -> p c t i", i=4),
+                z_bf[b][:, PACK * lo : PACK * hi].rearrange("p (c i t) -> p c t i", i=2, t=PACK),
+                charge[b][:, :, lo:hi].rearrange("p t (c i) -> p c t i", i=2),
+                develop[b][:, :, lo:hi].rearrange("p t (c i) -> p c t i", i=2),
                 ALU.add,
             )
 
-        def quantize_z(b):
-            nc.vector.quantize_mx(out=z_codes[b][:].bitcast(FP8X4), scales=z_scales[b][:], in_=z_bf[b][:])
+        def quantize_z(b, lo, hi):
+            nc.vector.quantize_mx(
+                out=z_codes[b][:, lo:hi].bitcast(FP8X4),
+                scales=z_scales[b][:, lo:hi],
+                in_=z_bf[b][:, PACK * lo : PACK * hi],
+            )
+
+        def widen_factors(b, slots):
+            for t in slots:
+                nc.scalar.copy(gain_wide[b][:, t, :], factors[:, t, b, 0:1].to_broadcast([P, M]))
+                nc.scalar.copy(product_wide[b][:, t, :], products[:, t, b : b + 1].to_broadcast([P, M]))
 
         gather_table(0, 0, S)
         cast_w1(nc.scalar.copy, 0, 0, 0, P)
         load_w1(0, 2)
         load_table(2)
         quantize_w1(0, 0)
+        widen_factors(0, range(PACK))
         cast_w1(nc.scalar.copy, 0, 1, 0, P)
         load_w1(1, 0)
         load_w1(1, 1)
         quantize_w1(0, 1)
         gather_table(1, 0, S)
+        widen_factors(1, range(2))
         cast_w1(nc.scalar.copy, 0, 2, 0, P)
         load_w1(1, 2)
         quantize_w1(0, 2)
@@ -203,9 +228,6 @@ def tile_list_drum_phase_scores_kernel(
 
         first_products(0)
 
-        for t in range(PACK):
-            nc.scalar.copy(gain_wide[0][:, t, :], factors[:, t, 0, 0:1].to_broadcast([P, M]))
-            nc.scalar.copy(product_wide[0][:, t, :], products[:, t, 0:1].to_broadcast([P, M]))
 
         pick_pairs(0, 0)
         pick_pairs(0, 1)
@@ -213,10 +235,10 @@ def tile_list_drum_phase_scores_kernel(
         w4_sb = streamed([P, PASSES2, 2 * N], U8, "c")
         nc.sync.dma_start(w4_sb[:].bitcast(I32), w4_words.bitcast(I32).rearrange("b p w -> p b w"))
         cap_rows = cap.rearrange("(j p) m -> p j m", p=P)
-        cap_sb = []
-        for j in range(0, N_TILES, 3):
-            cap_sb.append(w_stage[1][:, 0:3, :] if j == 0 else streamed([P, 3, M], F32, "b")[:])
-            nc.sync.dma_start(cap_sb[-1], cap_rows[:, j : j + 3, :])
+        cap_tail = streamed([P, 2, M], F32, "b")
+        nc.sync.dma_start(w_stage[1][:], cap_rows[:, 0:4, :])
+        nc.sync.dma_start(cap_tail[:], cap_rows[:, 4:6, :])
+        cap_sb = [w_stage[1][:, 0:2, :], w_stage[1][:, 2:4, :], cap_tail[:]]
         quantize_w1(1, 0)
         pick_pairs(0, 2)
         cast_w1(nc.scalar.copy, 1, 1, 0, P)
@@ -226,35 +248,60 @@ def tile_list_drum_phase_scores_kernel(
         cast_w1(nc.scalar.copy, 1, 2, P // 2, P)
         quantize_w1(1, 2)
         first_products(1)
-        for t in range(PACK):
-            nc.scalar.copy(product_wide[1][:, t, :], products[:, t, 1:2].to_broadcast([P, M]))
-        for pair in range(0, PACK, 2):
-            nc.vector.tensor_copy(
-                gain_wide[1][:, pair : pair + 2, :], factors[:, pair : pair + 2, 1, 0:1].to_broadcast([P, 2, M])
-            )
+        widen_factors(1, range(2, PACK))
         z_bf[0] = grouped[1, 2]
         z_bf[1] = ring.tile([P, M * PACK], BF16, name="grouped", align_bytes=64)
-        join(0)
+        join(0, 0, M)
         pick_pairs(1, 0)
-        quantize_z(0)
-        for t in range(1, PACK):
+        quantize_z(0, 0, M)
+        for t in range(1, PACK - 1):
             pick_pairs(1, t)
-        join(1)
-        quantize_z(1)
 
-        scores = [psum.tile([P, M], F32, name="bank") for j in range(N_TILES)]
-        for b in range(PASSES2):
-            for j in range(N_TILES):
-                nc.tensor.matmul_mx(
-                    out=scores[j][:],
-                    lhsT=w4_sb[:, b, 2 * P * j : 2 * P * (j + 1)].bitcast(FP4X4),
-                    lhsT_scale=w4_scale_sb[:, b, P * j : P * (j + 1)],
-                    rhs=z_codes[b][:].bitcast(FP8X4),
-                    rhs_scale=z_scales[b][:],
-                    start=(b == 0),
-                    stop=(b == PASSES2 - 1),
-                )
-        for j in range(N_TILES):
-            result = ring.tile([P, M], F32, name="result", bufs=N_TILES)
-            nc.vector.tensor_tensor(result[:], scores[j][:], cap_sb[j // 3][:, j % 3, :], ALU.min)
-            nc.sync.dma_start(out[P * j : P * (j + 1), :], result[:])
+        HM = M // 2
+        scores = {}
+
+        def second_product(b, half):
+            for pair in range(N_TILES // 2):
+                if b == 0:
+                    scores[half, pair] = psum.tile([P, 2, HM], F32, name="bank")
+                for side in range(2):
+                    j = 2 * pair + side
+                    for piece in range(HM // P):
+                        cols = slice(HM * half + P * piece, HM * half + P * (piece + 1))
+                        nc.tensor.matmul_mx(
+                            out=scores[half, pair][:, side, P * piece : P * (piece + 1)],
+                            lhsT=w4_sb[:, b, 2 * P * j : 2 * P * (j + 1)].bitcast(FP4X4),
+                            lhsT_scale=w4_scale_sb[:, b, P * j : P * (j + 1)],
+                            rhs=z_codes[b][:, cols].bitcast(FP8X4),
+                            rhs_scale=z_scales[b][:, cols],
+                            start=(b == 0 and side == 0 and piece == 0),
+                            stop=(b == PASSES2 - 1 and side == 1 and piece == HM // P - 1),
+                        )
+
+        out_rows = out.rearrange("(j p) m -> p j m", p=P)
+
+        def bound_and_store(half, pair):
+            cols = slice(HM * half, HM * (half + 1))
+            result = ring.tile([P, 2, HM], F32, name="result", bufs=N_TILES)
+            nc.vector.tensor_tensor(result[:], scores[half, pair][:], cap_sb[pair][:, :, cols], ALU.min)
+            nc.sync.dma_start(out_rows[:, 2 * pair : 2 * pair + 2, cols], result[:])
+
+        last = PACK - 1
+        leave_psum(1, last)
+        second_product(0, 0)
+        second_product(0, 1)
+        pick_charge(1, last, 0, HM)
+        pick_develop(1, last, 0, HM)
+        pick_charge(1, last, HM, M)
+        join(1, 0, HM)
+        pick_develop(1, last, HM, M)
+        quantize_z(1, 0, HM)
+        second_product(1, 0)
+        join(1, HM, M)
+        bound_and_store(0, 0)
+        quantize_z(1, HM, M)
+        second_product(1, 1)
+        for pair in range(1, N_TILES // 2):
+            bound_and_store(0, pair)
+        for pair in range(N_TILES // 2):
+            bound_and_store(1, pair)

@@ -70,24 +70,26 @@ def tile_list_drum_phase_scores_kernel(
             nc.sync.dma_start(table[a][:], tab_words[a].rearrange("p t i -> p (t i)").bitcast(I32))
 
         def load_w1(b, a):
-            if (b, a) == (1, 1):
+            if (b, a) == (1, 2):
                 w_raw[b, a] = streamed([P, PACK, K_PASS], F32, "b")
             else:
-                w_raw[b, a] = w_stage[(a + b) % 2 if b == 0 or a == 0 else 0]
+                w_raw[b, a] = w_stage[a + b]
             rows = w1[K_PASS * a : K_PASS * (a + 1), K_PASS * b : K_PASS * (b + 1)]
             nc.sync.dma_start(w_raw[b, a][:], rows.rearrange("(p j) c -> p j c", j=PACK))
 
         scale_window = streamed([P, T], U8, "b")
         warm = streamed([P, 2], F32, "c")
-        w_stage = [held([P, PACK, K_PASS], F32, "w_stage%d" % i) for i in range(2)]
+        w_stage = [held([P, PACK, K_PASS], F32, "w_stage%d" % i) for i in range(3)]
         warm_bias = w_stage[1][:, 0, 0:1]
+        warm_scale = w_stage[2][:, 0, 0:1]
         nc.vector.memset(warm[:, 0:1], 1.0)
         nc.vector.memset(factor_rows[:], 0.0)
         nc.vector.memset(scale_window[:].bitcast(I32), 0)
         nc.vector.memset(warm[:, 1:2], 1.0)
         nc.gpsimd.memset(warm_bias, 1.0)
+        nc.gpsimd.memset(warm_scale, 1.0)
         nc.gpsimd.memset(w4_scale_sb[:].rearrange("p b n -> p (b n)").bitcast(I32), 0)
-        nc.scalar.activation(warm[:], warm[:], ACT.Ln, bias=warm_bias)
+        nc.scalar.activation(warm[:], warm[:], ACT.Ln, bias=warm_bias, scale=warm_scale)
         nc.sync.dma_start(offs_sb[:], offs)
         nc.sync.dma_start(pos2_sb[:], pos2)
         nc.sync.dma_start(pos1_sb[:], pos1)
@@ -106,6 +108,7 @@ def tile_list_drum_phase_scores_kernel(
             nc.sync.dma_start(window32[4 + r : P : 16, :], scales32[1, r:16:2, :])
         load_table(0)
         load_w1(0, 1)
+        load_w1(0, 2)
         load_table(1)
 
         def gather_table(a, lo, hi):
@@ -197,28 +200,28 @@ def tile_list_drum_phase_scores_kernel(
                 in_=z_bf[b][:, PACK * lo : PACK * hi],
             )
 
-        def widen_factors(b, slots):
-            for t in slots:
-                nc.scalar.copy(gain_wide[b][:, t, :], factors[:, t, b, 0:1].to_broadcast([P, M]))
-                nc.scalar.copy(product_wide[b][:, t, :], products[:, t, b : b + 1].to_broadcast([P, M]))
-
         gather_table(0, 0, S)
-        cast_w1(nc.scalar.copy, 0, 0, 0, P)
-        load_w1(0, 2)
         load_table(2)
+        cast_w1(nc.scalar.copy, 0, 0, 0, P)
         quantize_w1(0, 0)
-        widen_factors(0, range(PACK))
         cast_w1(nc.scalar.copy, 0, 1, 0, P)
         load_w1(1, 0)
-        load_w1(1, 1)
         quantize_w1(0, 1)
-        gather_table(1, 0, S)
-        widen_factors(1, range(2))
         cast_w1(nc.scalar.copy, 0, 2, 0, P)
-        load_w1(1, 2)
+        load_w1(1, 1)
         quantize_w1(0, 2)
+        gather_table(1, 0, S)
+        load_w1(1, 2)
         gather_table(2, 0, BANK)
         gather_table(2, BANK, S)
+        for t in range(PACK):
+            nc.scalar.copy(gain_wide[0][:, t, :], factors[:, t, 0, 0:1].to_broadcast([P, M]))
+            nc.scalar.copy(product_wide[0][:, t, :], products[:, t, 0:1].to_broadcast([P, M]))
+        for pair in range(0, PACK, 2):
+            slots = slice(pair, pair + 2)
+            nc.vector.tensor_copy(gain_wide[1][:, slots, :], factors[:, slots, 1, 0:1].to_broadcast([P, 2, M]))
+            nc.vector.tensor_copy(product_wide[1][:, slots, :], products[:, slots, 1:2].to_broadcast([P, 2, M]))
+
         def first_products(b):
             for pair in range(0, PACK, 2):
                 for a in range(PASSES1):
@@ -235,20 +238,18 @@ def tile_list_drum_phase_scores_kernel(
         w4_sb = streamed([P, PASSES2, 2 * N], U8, "c")
         nc.sync.dma_start(w4_sb[:].bitcast(I32), w4_words.bitcast(I32).rearrange("b p w -> p b w"))
         cap_rows = cap.rearrange("(j p) m -> p j m", p=P)
-        cap_tail = streamed([P, 2, M], F32, "b")
         nc.sync.dma_start(w_stage[1][:], cap_rows[:, 0:4, :])
-        nc.sync.dma_start(cap_tail[:], cap_rows[:, 4:6, :])
-        cap_sb = [w_stage[1][:, 0:2, :], w_stage[1][:, 2:4, :], cap_tail[:]]
+        cap_sb = [w_stage[1][:, 0:2, :], w_stage[1][:, 2:4, :], w_stage[2][:, 0:2, :]]
         quantize_w1(1, 0)
         pick_pairs(0, 2)
         cast_w1(nc.scalar.copy, 1, 1, 0, P)
+        nc.sync.dma_start(cap_sb[2], cap_rows[:, 4:6, :])
         quantize_w1(1, 1)
         pick_pairs(0, 3)
         cast_w1(nc.vector.tensor_copy, 1, 2, 0, P // 2)
         cast_w1(nc.scalar.copy, 1, 2, P // 2, P)
         quantize_w1(1, 2)
         first_products(1)
-        widen_factors(1, range(2, PACK))
         z_bf[0] = grouped[1, 2]
         z_bf[1] = ring.tile([P, M * PACK], BF16, name="grouped", align_bytes=64)
         join(0, 0, M)

@@ -17,13 +17,16 @@ ALU = mybir.AluOpType
 ACT = mybir.ActivationFunctionType
 
 P = 128
+GROUP = 16
+QUADRANT = 32
 PACK = 4
-K_PASS = P * PACK
+PASS = P * PACK
 BANK = 512
-PASSES1 = K // K_PASS
-PASSES2 = H // K_PASS
-HALVES = S // BANK
-N_TILES = N // P
+K_PASSES = K // PASS
+R_PASSES = H // PASS
+S_HALVES = S // BANK
+N_PAIRS = N // (2 * P)
+M_HALF = M // 2
 
 
 def tile_list_drum_phase_scores_kernel(
@@ -38,48 +41,42 @@ def tile_list_drum_phase_scores_kernel(
         def held(shape, dtype, name):
             return keep.tile(shape, dtype, name=name, align_bytes=64)
 
-        offs_sb = held([P, S // 16], U16, "offs_sb")
-        pos1_sb = held([P, M // 16], U16, "pos1_sb")
-        pos2_sb = held([P, M // 16], U16, "pos2_sb")
+        offs_sb = held([P, S // GROUP], U16, "offs_sb")
+        pos1_sb = held([P, M // GROUP], U16, "pos1_sb")
+        pos2_sb = held([P, M // GROUP], U16, "pos2_sb")
         picked_scales = held([P, S], U8, "picked_scales")
         v_scales = held([P, S], U8, "v_scales")
-        table = {}
-        w_raw = {}
-        v_codes = [held([P, S], U32, "v_codes%d" % a) for a in range(PASSES1)]
-        w_keys = [(b, a) for b in range(PASSES2) for a in range(PASSES1)]
-        w_codes = {key: held([P, K_PASS], U32, "w_codes%d%d" % key) for key in w_keys}
-        w_scales = {key: held([P, K_PASS], U8, "w_scales%d%d" % key) for key in w_keys}
+        v_codes = [held([P, S], U32, "v_codes%d" % a) for a in range(K_PASSES)]
+        w_keys = [(b, a) for b in range(R_PASSES) for a in range(K_PASSES)]
+        w_codes = {key: held([P, PASS], U32, "w_codes%d%d" % key) for key in w_keys}
+        w_scales = {key: held([P, PASS], U8, "w_scales%d%d" % key) for key in w_keys}
         factor_rows = held([P, P], F32, "factor_rows")
         factor_dealt = held([P, P], F32, "factor_dealt")
-        factors = held([P, PACK, PASSES2, 16], F32, "factors")
-        products = held([P, PACK, PASSES2], F32, "products")
-        gain_wide = [held([P, PACK, M], F32, "gain_wide%d" % b) for b in range(PASSES2)]
-        product_wide = [held([P, PACK, M], F32, "product_wide%d" % b) for b in range(PASSES2)]
-        w4_scale_sb = held([P, PASSES2, N], U8, "w4_scale_sb")
-        charge = [held([P, PACK, M], F32, "charge%d" % b) for b in range(PASSES2)]
-        develop = [held([P, PACK, M], F32, "develop%d" % b) for b in range(PASSES2)]
-        z_codes = [held([P, M], U32, "z_codes%d" % b) for b in range(PASSES2)]
-        z_scales = [held([P, M], U8, "z_scales%d" % b) for b in range(PASSES2)]
+        factors = held([P, PACK, R_PASSES, GROUP], F32, "factors")
+        products = held([P, PACK, R_PASSES], F32, "products")
+        gain_wide = [held([P, PACK, M], F32, "gain_wide%d" % b) for b in range(R_PASSES)]
+        product_wide = [held([P, PACK, M], F32, "product_wide%d" % b) for b in range(R_PASSES)]
+        w4_scale_sb = held([P, R_PASSES, N], U8, "w4_scale_sb")
+        charge = [held([P, PACK, M], F32, "charge%d" % b) for b in range(R_PASSES)]
+        develop = [held([P, PACK, M], F32, "develop%d" % b) for b in range(R_PASSES)]
+        z_codes = [held([P, M], U32, "z_codes%d" % b) for b in range(R_PASSES)]
+        z_scales = [held([P, M], U8, "z_scales%d" % b) for b in range(R_PASSES)]
 
-
-        def streamed(shape, dtype, slot):
-            return keep.tile(shape, dtype, name="slot_" + slot, align_bytes=64)
+        table = {}
+        w_raw = {}
+        scale_window = held([P, T], U8, "lane_b")
+        warm = held([P, 2], F32, "lane_c")
+        w_stage = [held([P, PACK, PASS], F32, "w_stage%d" % i) for i in range(K_PASSES)]
 
         def load_table(a):
-            table[a] = streamed([P, T], I32, "cbc"[a])
+            table[a] = held([P, T], I32, "lane_b" if a == 1 else "lane_c")
             nc.sync.dma_start(table[a][:], tab_words[a].rearrange("p t i -> p (t i)").bitcast(I32))
 
         def load_w1(b, a):
-            if (b, a) == (1, 2):
-                w_raw[b, a] = streamed([P, PACK, K_PASS], F32, "b")
-            else:
-                w_raw[b, a] = w_stage[a + b]
-            rows = w1[K_PASS * a : K_PASS * (a + 1), K_PASS * b : K_PASS * (b + 1)]
+            w_raw[b, a] = w_stage[a + b] if a + b < K_PASSES else held([P, PACK, PASS], F32, "lane_b")
+            rows = w1[PASS * a : PASS * (a + 1), PASS * b : PASS * (b + 1)]
             nc.sync.dma_start(w_raw[b, a][:], rows.rearrange("(p j) c -> p j c", j=PACK))
 
-        scale_window = streamed([P, T], U8, "b")
-        warm = streamed([P, 2], F32, "c")
-        w_stage = [held([P, PACK, K_PASS], F32, "w_stage%d" % i) for i in range(3)]
         warm_bias = w_stage[1][:, 0, 0:1]
         warm_scale = w_stage[2][:, 0, 0:1]
         nc.vector.memset(warm[:, 0:1], 1.0)
@@ -90,92 +87,95 @@ def tile_list_drum_phase_scores_kernel(
         nc.gpsimd.memset(warm_scale, 1.0)
         nc.gpsimd.memset(w4_scale_sb[:].rearrange("p b n -> p (b n)").bitcast(I32), 0)
         nc.scalar.activation(warm[:], warm[:], ACT.Ln, bias=warm_bias, scale=warm_scale)
+
         nc.sync.dma_start(offs_sb[:], offs)
         nc.sync.dma_start(pos2_sb[:], pos2)
         nc.sync.dma_start(pos1_sb[:], pos1)
         load_w1(0, 0)
-        for v, vector in enumerate((gain, lift)):
-            nc.sync.dma_start(factor_rows[v:P:16, :], vector.rearrange("(b q c) -> q b c", b=PASSES2, c=P))
+
+        for which, vector in enumerate((gain, lift)):
+            nc.sync.dma_start(factor_rows[which:P:GROUP, :], vector.rearrange("(b d c) -> d b c", b=R_PASSES, c=P))
         nc.vector.tensor_copy(
             factor_dealt[:].rearrange("p (t i) -> p t i", t=PACK), factor_rows[:].rearrange("p (i t) -> p t i", t=PACK)
         )
-        nc.vector.transpose(factors[:].rearrange("p t b v -> p (t b v)"), factor_dealt[:])
+        nc.vector.transpose(factors[:].rearrange("p t b x -> p (t b x)"), factor_dealt[:])
         nc.vector.tensor_tensor(products[:], factors[:, :, :, 0], factors[:, :, :, 1], ALU.mult)
+
         window32 = scale_window[:].bitcast(I32)
         scales32 = tab_scales.bitcast(I32)
-        for r in range(2):
-            nc.sync.dma_start(window32[r:P:8, :], scales32[0:3:2, r:16:2, :].rearrange("a g w -> g a w"))
-            nc.sync.dma_start(window32[4 + r : P : 16, :], scales32[1, r:16:2, :])
+        for i in range(2):
+            nc.sync.dma_start(window32[i:P:8, :], scales32[0:3:2, i:16:2, :].rearrange("a g w -> g a w"))
+            nc.sync.dma_start(window32[PACK + i : P : GROUP, :], scales32[1, i:16:2, :])
         load_table(0)
         load_w1(0, 1)
         load_w1(0, 2)
         load_table(1)
 
-        def gather_table(a, lo, hi):
-            nc.vector.tensor_copy(
-                v_codes[a][:, lo:hi], table[a][:].bitcast(U32).indirect(offs_sb[:, lo // 16 : hi // 16])
-            )
-
         nc.vector.tensor_copy(picked_scales[:], scale_window[:].indirect(offs_sb[:]))
         picked32 = picked_scales[:].bitcast(I32)
         planes32 = v_scales[:].bitcast(I32)
         nc.vector.tensor_copy(planes32, picked32)
-        for r in range(2):
-            nc.sync.dma_start(planes32[2 + r : P - 14 + r : 4, :], picked32[16 + r : P : 4, :])
-        for d in range(4):
+        for i in range(2):
+            nc.sync.dma_start(planes32[2 + i : 2 + P - GROUP + i : PACK, :], picked32[GROUP + i : P : PACK, :])
+
+        for d in range(P // QUADRANT):
             nc.gpsimd.dma_start(
-                w4_scale_sb[:].bitcast(I32)[32 * d : 32 * d + 4],
-                w4_scales.bitcast(I32)[:, 4 * d : 4 * d + 4, :].rearrange("b r w -> r b w"),
+                w4_scale_sb[:].bitcast(I32)[QUADRANT * d : QUADRANT * d + PACK],
+                w4_scales.bitcast(I32)[:, PACK * d : PACK * (d + 1), :].rearrange("b i w -> i b w"),
             )
 
-        probe = held([P, 16], F32, "probe")
+        def gather_table(a, lo, hi):
+            picked = table[a][:].bitcast(U32).indirect(offs_sb[:, lo // GROUP : hi // GROUP])
+            nc.vector.tensor_copy(v_codes[a][:, lo:hi], picked)
+
         grouped = {}
 
-        def cast_w1(copy, b, a, lo, hi):
-            if (b, a) not in grouped:
-                grouped[b, a] = ring.tile([P, PACK * K_PASS], BF16, name="grouped", align_bytes=64)
-            dst = grouped[b, a][:].rearrange("p (t m j) -> p m j t", t=PACK, j=PACK)
-            src = w_raw[b, a][:].rearrange("p j (m t) -> p m j t", t=PACK)
-            copy(dst[:, lo:hi], src[:, lo:hi])
+        def cast_w1(copy, b, a, lo=0, hi=P):
+            if lo == 0:
+                grouped[b, a] = ring.tile([P, PACK * PASS], BF16, name="grouped", align_bytes=64)
+            dealt = grouped[b, a][:].rearrange("p (t m j) -> p m j t", t=PACK, j=PACK)
+            copy(dealt[:, lo:hi], w_raw[b, a][:].rearrange("p j (m t) -> p m j t", t=PACK)[:, lo:hi])
 
         def quantize_w1(b, a):
             nc.vector.quantize_mx(out=w_codes[b, a][:].bitcast(FP8X4), scales=w_scales[b, a][:], in_=grouped[b, a][:])
 
         banks = {}
 
-        def first_product(b, t, half, a):
-            if a == 0:
-                banks[b, t, half] = psum.tile([P, BANK], F32, name="bank")
-            rows = slice(P * t, P * (t + 1))
-            cols = slice(BANK * half, BANK * (half + 1))
-            nc.tensor.matmul_mx(
-                out=banks[b, t, half][:],
-                lhsT=w_codes[b, a][:, rows].bitcast(FP8X4),
-                lhsT_scale=w_scales[b, a][:, rows],
-                rhs=v_codes[a][:, cols].bitcast(FP8X4),
-                rhs_scale=v_scales[4 * a : P, cols],
-                start=(a == 0),
-                stop=(a == PASSES1 - 1),
-            )
+        def first_products(b):
+            for pair in range(0, PACK, 2):
+                for a in range(K_PASSES):
+                    for t in (pair, pair + 1):
+                        for half in range(S_HALVES):
+                            if a == 0:
+                                banks[b, t, half] = psum.tile([P, BANK], F32, name="bank")
+                            rows = slice(P * t, P * (t + 1))
+                            cols = slice(BANK * half, BANK * (half + 1))
+                            nc.tensor.matmul_mx(
+                                out=banks[b, t, half][:],
+                                lhsT=w_codes[b, a][:, rows].bitcast(FP8X4),
+                                lhsT_scale=w_scales[b, a][:, rows],
+                                rhs=v_codes[a][:, cols].bitcast(FP8X4),
+                                rhs_scale=v_scales[PACK * a : P, cols],
+                                start=(a == 0),
+                                stop=(a == K_PASSES - 1),
+                            )
 
         strength = {}
         logged = {}
 
         def leave_psum(b, t):
             strength[b, t] = ring.tile([P, S], F32, name="strength", bufs=4)
-            for half in range(HALVES):
+            for half in range(S_HALVES):
                 nc.scalar.activation(strength[b, t][:, BANK * half : BANK * (half + 1)], banks[b, t, half][:], ACT.Abs)
-            if t == 0:
-                nc.gpsimd.tensor_copy(probe[:, b : b + 1], strength[b, t][:, S - 1 : S])
             logged[b, t] = ring.tile([P, S], F32, name="logged")
             nc.scalar.activation(logged[b, t][:], strength[b, t][:], ACT.Ln, bias=1.0)
 
         def pick_charge(b, t, lo, hi):
-            picked = strength[b, t][:].indirect(pos1_sb[:, lo // 16 : hi // 16])
+            picked = strength[b, t][:].indirect(pos1_sb[:, lo // GROUP : hi // GROUP])
             nc.vector.tensor_tensor(charge[b][:, t, lo:hi], picked, gain_wide[b][:, t, lo:hi], ALU.mult)
 
         def pick_develop(b, t, lo, hi):
-            picked = logged[b, t][:].indirect(pos2_sb[:, lo // 16 : hi // 16])
+            picked = logged[b, t][:].indirect(pos2_sb[:, lo // GROUP : hi // GROUP])
             nc.vector.tensor_tensor(develop[b][:, t, lo:hi], picked, product_wide[b][:, t, lo:hi], ALU.mult)
 
         def pick_pairs(b, t):
@@ -200,49 +200,43 @@ def tile_list_drum_phase_scores_kernel(
                 in_=z_bf[b][:, PACK * lo : PACK * hi],
             )
 
+        def widen_factors(copy, b, lo, hi):
+            shape = [P, hi - lo, M]
+            copy(gain_wide[b][:, lo:hi, :], factors[:, lo:hi, b, 0:1].to_broadcast(shape))
+            copy(product_wide[b][:, lo:hi, :], products[:, lo:hi, b : b + 1].to_broadcast(shape))
+
         gather_table(0, 0, S)
         load_table(2)
-        cast_w1(nc.scalar.copy, 0, 0, 0, P)
+        cast_w1(nc.scalar.copy, 0, 0)
         quantize_w1(0, 0)
-        cast_w1(nc.scalar.copy, 0, 1, 0, P)
+        cast_w1(nc.scalar.copy, 0, 1)
         load_w1(1, 0)
         quantize_w1(0, 1)
-        cast_w1(nc.scalar.copy, 0, 2, 0, P)
+        cast_w1(nc.scalar.copy, 0, 2)
         load_w1(1, 1)
         quantize_w1(0, 2)
         gather_table(1, 0, S)
         load_w1(1, 2)
         gather_table(2, 0, BANK)
         gather_table(2, BANK, S)
+
         for t in range(PACK):
-            nc.scalar.copy(gain_wide[0][:, t, :], factors[:, t, 0, 0:1].to_broadcast([P, M]))
-            nc.scalar.copy(product_wide[0][:, t, :], products[:, t, 0:1].to_broadcast([P, M]))
+            widen_factors(nc.scalar.copy, 0, t, t + 1)
         for pair in range(0, PACK, 2):
-            slots = slice(pair, pair + 2)
-            nc.vector.tensor_copy(gain_wide[1][:, slots, :], factors[:, slots, 1, 0:1].to_broadcast([P, 2, M]))
-            nc.vector.tensor_copy(product_wide[1][:, slots, :], products[:, slots, 1:2].to_broadcast([P, 2, M]))
-
-        def first_products(b):
-            for pair in range(0, PACK, 2):
-                for a in range(PASSES1):
-                    for t in (pair, pair + 1):
-                        for half in range(HALVES):
-                            first_product(b, t, half, a)
-
+            widen_factors(nc.vector.tensor_copy, 1, pair, pair + 2)
         first_products(0)
-
 
         pick_pairs(0, 0)
         pick_pairs(0, 1)
-        cast_w1(nc.vector.tensor_copy, 1, 0, 0, P)
-        w4_sb = streamed([P, PASSES2, 2 * N], U8, "c")
+        cast_w1(nc.vector.tensor_copy, 1, 0)
+        w4_sb = held([P, R_PASSES, 2 * N], U8, "lane_c")
         nc.sync.dma_start(w4_sb[:].bitcast(I32), w4_words.bitcast(I32).rearrange("b p w -> p b w"))
         cap_rows = cap.rearrange("(j p) m -> p j m", p=P)
-        nc.sync.dma_start(w_stage[1][:], cap_rows[:, 0:4, :])
         cap_sb = [w_stage[1][:, 0:2, :], w_stage[1][:, 2:4, :], w_stage[2][:, 0:2, :]]
+        nc.sync.dma_start(w_stage[1][:], cap_rows[:, 0:4, :])
         quantize_w1(1, 0)
         pick_pairs(0, 2)
-        cast_w1(nc.scalar.copy, 1, 1, 0, P)
+        cast_w1(nc.scalar.copy, 1, 1)
         nc.sync.dma_start(cap_sb[2], cap_rows[:, 4:6, :])
         quantize_w1(1, 1)
         pick_pairs(0, 3)
@@ -250,7 +244,8 @@ def tile_list_drum_phase_scores_kernel(
         cast_w1(nc.scalar.copy, 1, 2, P // 2, P)
         quantize_w1(1, 2)
         first_products(1)
-        z_bf[0] = grouped[1, 2]
+
+        z_bf[0] = grouped[1, K_PASSES - 1]
         z_bf[1] = ring.tile([P, M * PACK], BF16, name="grouped", align_bytes=64)
         join(0, 0, M)
         pick_pairs(1, 0)
@@ -258,17 +253,17 @@ def tile_list_drum_phase_scores_kernel(
         for t in range(1, PACK - 1):
             pick_pairs(1, t)
 
-        HM = M // 2
         scores = {}
 
         def second_product(b, half):
-            for pair in range(N_TILES // 2):
+            pieces = M_HALF // P
+            for pair in range(N_PAIRS):
                 if b == 0:
-                    scores[half, pair] = psum.tile([P, 2, HM], F32, name="bank")
+                    scores[half, pair] = psum.tile([P, 2, M_HALF], F32, name="bank")
                 for side in range(2):
                     j = 2 * pair + side
-                    for piece in range(HM // P):
-                        cols = slice(HM * half + P * piece, HM * half + P * (piece + 1))
+                    for piece in range(pieces):
+                        cols = slice(M_HALF * half + P * piece, M_HALF * half + P * (piece + 1))
                         nc.tensor.matmul_mx(
                             out=scores[half, pair][:, side, P * piece : P * (piece + 1)],
                             lhsT=w4_sb[:, b, 2 * P * j : 2 * P * (j + 1)].bitcast(FP4X4),
@@ -276,14 +271,14 @@ def tile_list_drum_phase_scores_kernel(
                             rhs=z_codes[b][:, cols].bitcast(FP8X4),
                             rhs_scale=z_scales[b][:, cols],
                             start=(b == 0 and side == 0 and piece == 0),
-                            stop=(b == PASSES2 - 1 and side == 1 and piece == HM // P - 1),
+                            stop=(b == R_PASSES - 1 and side == 1 and piece == pieces - 1),
                         )
 
         out_rows = out.rearrange("(j p) m -> p j m", p=P)
 
         def bound_and_store(half, pair):
-            cols = slice(HM * half, HM * (half + 1))
-            result = ring.tile([P, 2, HM], F32, name="result", bufs=N_TILES)
+            cols = slice(M_HALF * half, M_HALF * (half + 1))
+            result = ring.tile([P, 2, M_HALF], F32, name="result", bufs=2 * N_PAIRS)
             nc.vector.tensor_tensor(result[:], scores[half, pair][:], cap_sb[pair][:, :, cols], ALU.min)
             nc.sync.dma_start(out_rows[:, 2 * pair : 2 * pair + 2, cols], result[:])
 
@@ -291,18 +286,18 @@ def tile_list_drum_phase_scores_kernel(
         leave_psum(1, last)
         second_product(0, 0)
         second_product(0, 1)
-        pick_charge(1, last, 0, HM)
-        pick_develop(1, last, 0, HM)
-        pick_charge(1, last, HM, M)
-        join(1, 0, HM)
-        pick_develop(1, last, HM, M)
-        quantize_z(1, 0, HM)
+        pick_charge(1, last, 0, M_HALF)
+        pick_develop(1, last, 0, M_HALF)
+        pick_charge(1, last, M_HALF, M)
+        join(1, 0, M_HALF)
+        pick_develop(1, last, M_HALF, M)
+        quantize_z(1, 0, M_HALF)
         second_product(1, 0)
-        join(1, HM, M)
+        join(1, M_HALF, M)
         bound_and_store(0, 0)
-        quantize_z(1, HM, M)
+        quantize_z(1, M_HALF, M)
         second_product(1, 1)
-        for pair in range(1, N_TILES // 2):
+        for pair in range(1, N_PAIRS):
             bound_and_store(0, pair)
-        for pair in range(N_TILES // 2):
+        for pair in range(N_PAIRS):
             bound_and_store(1, pair)

from contextlib import ExitStack

import concourse.mybir as mybir

K, H, N, T, S, M = 1536, 1024, 768, 2048, 1024, 512
FLOPS = 2 * K * H * S + 2 * H * N * M

F32 = mybir.dt.float32
BF16 = mybir.dt.bfloat16
I32 = mybir.dt.int32
U32 = mybir.dt.uint32
U16 = mybir.dt.uint16
U8 = mybir.dt.uint8
FP8X4 = mybir.dt.float8_e4m3fn_x4
FP4X4 = mybir.dt.float4_e2m1fn_x4
ALU = mybir.AluOpType
ACT = mybir.ActivationFunctionType

P = 128
GROUP = 16
QUADRANT = 32
PACK = 4
PASS = P * PACK
BANK = 512
K_PASSES = K // PASS
R_PASSES = H // PASS
S_HALVES = S // BANK
N_PAIRS = N // (2 * P)
M_HALF = M // 2


def tile_list_drum_phase_scores_kernel(
    tc, tab_words, tab_scales, offs, pos1, pos2, w1, lift, gain, w4_words, w4_scales, cap, out
):
    nc = tc.nc
    with ExitStack() as ctx:
        keep = ctx.enter_context(tc.tile_pool(name="keep", bufs=1))
        ring = ctx.enter_context(tc.tile_pool(name="ring", bufs=3))
        psum = ctx.enter_context(tc.psum_pool(name="psum", bufs=8))

        def held(shape, dtype, name):
            return keep.tile(shape, dtype, name=name, align_bytes=64)

        offs_sb = held([P, S // GROUP], U16, "offs_sb")
        pos1_sb = held([P, M // GROUP], U16, "pos1_sb")
        pos2_sb = held([P, M // GROUP], U16, "pos2_sb")
        picked_scales = held([P, S], U8, "picked_scales")
        v_scales = held([P, S], U8, "v_scales")
        v_codes = [held([P, S], U32, "v_codes%d" % a) for a in range(K_PASSES)]
        w_keys = [(b, a) for b in range(R_PASSES) for a in range(K_PASSES)]
        w_codes = {key: held([P, PASS], U32, "w_codes%d%d" % key) for key in w_keys}
        w_scales = {key: held([P, PASS], U8, "w_scales%d%d" % key) for key in w_keys}
        factor_rows = held([P, P], F32, "factor_rows")
        factor_dealt = held([P, P], F32, "factor_dealt")
        factors = held([P, PACK, R_PASSES, GROUP], F32, "factors")
        products = held([P, PACK, R_PASSES], F32, "products")
        gain_wide = [held([P, PACK, M], F32, "gain_wide%d" % b) for b in range(R_PASSES)]
        product_wide = [held([P, PACK, M], F32, "product_wide%d" % b) for b in range(R_PASSES)]
        w4_scale_sb = held([P, R_PASSES, N], U8, "w4_scale_sb")
        charge = [held([P, PACK, M], F32, "charge%d" % b) for b in range(R_PASSES)]
        develop = [held([P, PACK, M], F32, "develop%d" % b) for b in range(R_PASSES)]
        z_codes = [held([P, M], U32, "z_codes%d" % b) for b in range(R_PASSES)]
        z_scales = [held([P, M], U8, "z_scales%d" % b) for b in range(R_PASSES)]

        table = {}
        w_raw = {}
        scale_window = held([P, T], U8, "lane_b")
        warm = held([P, 2], F32, "lane_c")
        w_stage = [held([P, PACK, PASS], F32, "w_stage%d" % i) for i in range(K_PASSES)]

        def load_table(a):
            table[a] = held([P, T], I32, "lane_b" if a == 1 else "lane_c")
            nc.sync.dma_start(table[a][:], tab_words[a].rearrange("p t i -> p (t i)").bitcast(I32))

        def load_w1(b, a):
            w_raw[b, a] = w_stage[a + b] if a + b < K_PASSES else held([P, PACK, PASS], F32, "lane_b")
            rows = w1[PASS * a : PASS * (a + 1), PASS * b : PASS * (b + 1)]
            nc.sync.dma_start(w_raw[b, a][:], rows.rearrange("(p j) c -> p j c", j=PACK))

        warm_bias = w_stage[1][:, 0, 0:1]
        warm_scale = w_stage[2][:, 0, 0:1]
        nc.vector.memset(warm[:, 0:1], 1.0)
        nc.vector.memset(factor_rows[:], 0.0)
        nc.vector.memset(scale_window[:].bitcast(I32), 0)
        nc.vector.memset(warm[:, 1:2], 1.0)
        nc.gpsimd.memset(warm_bias, 1.0)
        nc.gpsimd.memset(warm_scale, 1.0)
        nc.gpsimd.memset(w4_scale_sb[:].rearrange("p b n -> p (b n)").bitcast(I32), 0)
        nc.scalar.activation(warm[:], warm[:], ACT.Ln, bias=warm_bias, scale=warm_scale)

        nc.sync.dma_start(offs_sb[:], offs)
        nc.sync.dma_start(pos2_sb[:], pos2)
        nc.sync.dma_start(pos1_sb[:], pos1)
        load_w1(0, 0)

        for which, vector in enumerate((gain, lift)):
            nc.sync.dma_start(factor_rows[which:P:GROUP, :], vector.rearrange("(b d c) -> d b c", b=R_PASSES, c=P))
        nc.vector.tensor_copy(
            factor_dealt[:].rearrange("p (t i) -> p t i", t=PACK), factor_rows[:].rearrange("p (i t) -> p t i", t=PACK)
        )
        nc.vector.transpose(factors[:].rearrange("p t b x -> p (t b x)"), factor_dealt[:])
        nc.vector.tensor_tensor(products[:], factors[:, :, :, 0], factors[:, :, :, 1], ALU.mult)

        window32 = scale_window[:].bitcast(I32)
        scales32 = tab_scales.bitcast(I32)
        for i in range(2):
            nc.sync.dma_start(window32[i:P:8, :], scales32[0:3:2, i:16:2, :].rearrange("a g w -> g a w"))
            nc.sync.dma_start(window32[PACK + i : P : GROUP, :], scales32[1, i:16:2, :])
        load_table(0)
        load_w1(0, 1)
        load_w1(0, 2)
        load_table(1)

        nc.vector.tensor_copy(picked_scales[:], scale_window[:].indirect(offs_sb[:]))
        picked32 = picked_scales[:].bitcast(I32)
        planes32 = v_scales[:].bitcast(I32)
        nc.vector.tensor_copy(planes32, picked32)
        for i in range(2):
            nc.sync.dma_start(planes32[2 + i : 2 + P - GROUP + i : PACK, :], picked32[GROUP + i : P : PACK, :])

        for d in range(P // QUADRANT):
            nc.gpsimd.dma_start(
                w4_scale_sb[:].bitcast(I32)[QUADRANT * d : QUADRANT * d + PACK],
                w4_scales.bitcast(I32)[:, PACK * d : PACK * (d + 1), :].rearrange("b i w -> i b w"),
            )

        def gather_table(a, lo, hi):
            picked = table[a][:].bitcast(U32).indirect(offs_sb[:, lo // GROUP : hi // GROUP])
            nc.vector.tensor_copy(v_codes[a][:, lo:hi], picked)

        grouped = {}

        def cast_w1(copy, b, a, lo=0, hi=P):
            if lo == 0:
                grouped[b, a] = ring.tile([P, PACK * PASS], BF16, name="grouped", align_bytes=64)
            dealt = grouped[b, a][:].rearrange("p (t m j) -> p m j t", t=PACK, j=PACK)
            copy(dealt[:, lo:hi], w_raw[b, a][:].rearrange("p j (m t) -> p m j t", t=PACK)[:, lo:hi])

        def quantize_w1(b, a):
            nc.vector.quantize_mx(out=w_codes[b, a][:].bitcast(FP8X4), scales=w_scales[b, a][:], in_=grouped[b, a][:])

        banks = {}

        def first_products(b):
            for pair in range(0, PACK, 2):
                for a in range(K_PASSES):
                    for t in (pair, pair + 1):
                        for half in range(S_HALVES):
                            if a == 0:
                                banks[b, t, half] = psum.tile([P, BANK], F32, name="bank")
                            rows = slice(P * t, P * (t + 1))
                            cols = slice(BANK * half, BANK * (half + 1))
                            nc.tensor.matmul_mx(
                                out=banks[b, t, half][:],
                                lhsT=w_codes[b, a][:, rows].bitcast(FP8X4),
                                lhsT_scale=w_scales[b, a][:, rows],
                                rhs=v_codes[a][:, cols].bitcast(FP8X4),
                                rhs_scale=v_scales[PACK * a : P, cols],
                                start=(a == 0),
                                stop=(a == K_PASSES - 1),
                            )

        strength = {}
        logged = {}

        def leave_psum(b, t):
            strength[b, t] = ring.tile([P, S], F32, name="strength", bufs=4)
            for half in range(S_HALVES):
                nc.scalar.activation(strength[b, t][:, BANK * half : BANK * (half + 1)], banks[b, t, half][:], ACT.Abs)
            logged[b, t] = ring.tile([P, S], F32, name="logged")
            nc.scalar.activation(logged[b, t][:], strength[b, t][:], ACT.Ln, bias=1.0)

        def pick_charge(b, t, lo, hi):
            picked = strength[b, t][:].indirect(pos1_sb[:, lo // GROUP : hi // GROUP])
            nc.vector.tensor_tensor(charge[b][:, t, lo:hi], picked, gain_wide[b][:, t, lo:hi], ALU.mult)

        def pick_develop(b, t, lo, hi):
            picked = logged[b, t][:].indirect(pos2_sb[:, lo // GROUP : hi // GROUP])
            nc.vector.tensor_tensor(develop[b][:, t, lo:hi], picked, product_wide[b][:, t, lo:hi], ALU.mult)

        def pick_pairs(b, t):
            leave_psum(b, t)
            pick_charge(b, t, 0, M)
            pick_develop(b, t, 0, M)

        z_bf = {}

        def join(b, lo, hi):
            nc.vector.tensor_tensor(
                z_bf[b][:, PACK * lo : PACK * hi].rearrange("p (c i t) -> p c t i", i=2, t=PACK),
                charge[b][:, :, lo:hi].rearrange("p t (c i) -> p c t i", i=2),
                develop[b][:, :, lo:hi].rearrange("p t (c i) -> p c t i", i=2),
                ALU.add,
            )

        def quantize_z(b, lo, hi):
            nc.vector.quantize_mx(
                out=z_codes[b][:, lo:hi].bitcast(FP8X4),
                scales=z_scales[b][:, lo:hi],
                in_=z_bf[b][:, PACK * lo : PACK * hi],
            )

        def widen_factors(copy, b, lo, hi):
            shape = [P, hi - lo, M]
            copy(gain_wide[b][:, lo:hi, :], factors[:, lo:hi, b, 0:1].to_broadcast(shape))
            copy(product_wide[b][:, lo:hi, :], products[:, lo:hi, b : b + 1].to_broadcast(shape))

        gather_table(0, 0, S)
        load_table(2)
        cast_w1(nc.scalar.copy, 0, 0)
        quantize_w1(0, 0)
        cast_w1(nc.scalar.copy, 0, 1)
        load_w1(1, 0)
        quantize_w1(0, 1)
        cast_w1(nc.scalar.copy, 0, 2)
        load_w1(1, 1)
        quantize_w1(0, 2)
        gather_table(1, 0, S)
        load_w1(1, 2)
        gather_table(2, 0, BANK)
        gather_table(2, BANK, S)

        for t in range(PACK):
            widen_factors(nc.scalar.copy, 0, t, t + 1)
        for pair in range(0, PACK, 2):
            widen_factors(nc.vector.tensor_copy, 1, pair, pair + 2)
        first_products(0)

        pick_pairs(0, 0)
        pick_pairs(0, 1)
        cast_w1(nc.vector.tensor_copy, 1, 0)
        w4_sb = held([P, R_PASSES, 2 * N], U8, "lane_c")
        nc.sync.dma_start(w4_sb[:].bitcast(I32), w4_words.bitcast(I32).rearrange("b p w -> p b w"))
        cap_rows = cap.rearrange("(j p) m -> p j m", p=P)
        cap_sb = [w_stage[1][:, 0:2, :], w_stage[1][:, 2:4, :], w_stage[2][:, 0:2, :]]
        nc.sync.dma_start(w_stage[1][:], cap_rows[:, 0:4, :])
        quantize_w1(1, 0)
        pick_pairs(0, 2)
        cast_w1(nc.scalar.copy, 1, 1)
        nc.sync.dma_start(cap_sb[2], cap_rows[:, 4:6, :])
        quantize_w1(1, 1)
        pick_pairs(0, 3)
        cast_w1(nc.vector.tensor_copy, 1, 2, 0, P // 2)
        cast_w1(nc.scalar.copy, 1, 2, P // 2, P)
        quantize_w1(1, 2)
        first_products(1)

        z_bf[0] = grouped[1, K_PASSES - 1]
        z_bf[1] = ring.tile([P, M * PACK], BF16, name="grouped", align_bytes=64)
        join(0, 0, M)
        pick_pairs(1, 0)
        quantize_z(0, 0, M)
        for t in range(1, PACK - 1):
            pick_pairs(1, t)

        scores = {}

        def second_product(b, half):
            pieces = M_HALF // P
            for pair in range(N_PAIRS):
                if b == 0:
                    scores[half, pair] = psum.tile([P, 2, M_HALF], F32, name="bank")
                for side in range(2):
                    j = 2 * pair + side
                    for piece in range(pieces):
                        cols = slice(M_HALF * half + P * piece, M_HALF * half + P * (piece + 1))
                        nc.tensor.matmul_mx(
                            out=scores[half, pair][:, side, P * piece : P * (piece + 1)],
                            lhsT=w4_sb[:, b, 2 * P * j : 2 * P * (j + 1)].bitcast(FP4X4),
                            lhsT_scale=w4_scale_sb[:, b, P * j : P * (j + 1)],
                            rhs=z_codes[b][:, cols].bitcast(FP8X4),
                            rhs_scale=z_scales[b][:, cols],
                            start=(b == 0 and side == 0 and piece == 0),
                            stop=(b == R_PASSES - 1 and side == 1 and piece == pieces - 1),
                        )

        out_rows = out.rearrange("(j p) m -> p j m", p=P)

        def bound_and_store(half, pair):
            cols = slice(M_HALF * half, M_HALF * (half + 1))
            result = ring.tile([P, 2, M_HALF], F32, name="result", bufs=2 * N_PAIRS)
            nc.vector.tensor_tensor(result[:], scores[half, pair][:], cap_sb[pair][:, :, cols], ALU.min)
            nc.sync.dma_start(out_rows[:, 2 * pair : 2 * pair + 2, cols], result[:])

        last = PACK - 1
        leave_psum(1, last)
        second_product(0, 0)
        second_product(0, 1)
        pick_charge(1, last, 0, M_HALF)
        pick_develop(1, last, 0, M_HALF)
        pick_charge(1, last, M_HALF, M)
        join(1, 0, M_HALF)
        pick_develop(1, last, M_HALF, M)
        quantize_z(1, 0, M_HALF)
        second_product(1, 0)
        join(1, M_HALF, M)
        bound_and_store(0, 0)
        quantize_z(1, M_HALF, M)
        second_product(1, 1)
        for pair in range(1, N_PAIRS):
            bound_and_store(0, pair)
        for pair in range(N_PAIRS):
            bound_and_store(1, pair)
